import numpy as np
import ml_dtypes


def mxq(x, axis, fmt="e4m3"):
    dtype, down = {"e4m3": (ml_dtypes.float8_e4m3fn, 7), "e5m2": (ml_dtypes.float8_e5m2, 14)}[fmt]
    v = np.moveaxis(np.asarray(x, np.float32).astype(ml_dtypes.bfloat16).astype(np.float64), axis, -1)
    blocks = v.reshape(v.shape[:-1] + (-1, 32))
    amax = np.abs(blocks).max(-1, keepdims=True)
    byte = np.maximum(np.where(amax > 0, np.frexp(amax)[1] - 1 + 127, 0) - down, 1)
    scale = np.exp2(byte - 127.0)
    codes = (blocks / scale).astype(np.float32).astype(dtype).astype(np.float64)
    return np.moveaxis((codes * scale).reshape(v.shape), -1, axis)


WIDE = False


def mx_kscale(k):
    if not WIDE:
        return np.ones(k)
    levels = np.array([10, -10, 5, -5, 0])
    if k % 512:
        return np.exp2(np.random.permutation(np.resize(levels, k // 32))).repeat(32)
    a = np.empty((k // 512, 16))
    for p in range(k // 512):
        a[p, :8] = np.random.permutation(np.resize(levels, 8))
        for g in range(8):
            far = levels[np.abs(levels - a[p, g]) >= 10]
            a[p, g + 8] = far[np.random.randint(len(far))]
    return np.exp2(a.ravel()).repeat(32)


def f64(x):
    return np.asarray(x).astype(np.float64)


def striped(idx):
    return np.tile(idx.reshape(-1, 16).T, (8, 1)).astype(np.uint16)


def unstriped(offs):
    return offs[:16].T.reshape(-1).astype(np.int64)


def striped8(idx):
    return np.concatenate([x.reshape(-1, 16).T for x in idx]).astype(np.uint16)


def runs(offs, k):
    lists = np.stack([offs[16 * r : 16 * r + 16].T.reshape(-1) for r in range(8)]).astype(np.int64)
    return lists[np.arange(k) % 512 // 64]


def pack_weight(w):
    k, n = w.shape
    w = f64(np.asarray(w, np.float32).astype(ml_dtypes.bfloat16)).reshape(k // 32, 32, n)
    amax = np.abs(w).max(1)
    byte = np.clip(np.where(amax > 0, np.frexp(amax)[1] - 1 + 127 - 7, 1), 1, 254)
    scaled = (w * np.exp2(127.0 - byte)[:, None, :]).reshape(k, n).astype(np.float32)
    words = np.ascontiguousarray(scaled.reshape(k // 512, 128, 4, n).transpose(0, 1, 3, 2)).astype(ml_dtypes.float8_e4m3fn).view(np.uint8)
    return words, np.ascontiguousarray(byte.astype(np.uint8).reshape(k // 512, 16, n))


def unpack_weight(words, scales):
    g, p, n, _ = words.shape
    vals = np.ascontiguousarray(words).view(ml_dtypes.float8_e4m3fn).astype(np.float64) * np.repeat(np.exp2(scales.astype(np.float64) - 127.0), 8, axis=1)[..., None]
    return vals.transpose(0, 1, 3, 2).reshape(g * 512, n)


K, T, S, N, G, H, W = 512, 1024, 512, 512, 2048, 512, 256


def setup_inputs():
    n = np.random.standard_normal
    s = mx_kscale(K)[:, None]
    u = mx_kscale(S)
    packed_xT = pack_weight(n((K, T)) * s)
    packed_dT = pack_weight(n((K, G)) / s)
    perm = np.stack([np.random.permutation(S) for _ in range(8)])
    return {
        "x_words": packed_xT[0],
        "x_scales": packed_xT[1],
        "d_words": packed_dT[0],
        "d_scales": packed_dT[1],
        "gn": (np.random.uniform(0.5, 1.5, (H, 1)) * u[:, None]).astype(np.float32),
        "w1": (n((H, N)) / np.sqrt(H) / u[:, None]).astype(np.float32),
        "offs": striped(np.random.permutation(T)[:S]),
        "k1": striped8(np.random.randint(0, G, (8, H))),
        "two": striped(np.random.permutation(T)[:S]),
        "k2": striped8(np.random.randint(0, G, (8, H))),
        "n1": striped8(np.stack([np.random.permutation(S) for _ in range(8)])),
        "n2": striped8(np.stack([np.random.permutation(S) for _ in range(8)])),
        "n3": striped8(np.stack([np.random.permutation(S) for _ in range(8)])),
        "n4": striped8(np.stack([np.random.permutation(S) for _ in range(8)])),
        "n5": striped8(perm[:, :W]),
        "n6": striped8(perm[:, W:]),
    }


def reference(x_words, x_scales, d_words, d_scales, gn, w1, offs, k1, two, k2, n1, n2, n3, n4, n5, n6):
    d_k1 = unpack_weight(d_words, d_scales)[np.arange(K)[:, None], runs(k1, K)]
    xq = unpack_weight(x_words, x_scales)[:, unstriped(offs)]
    a = 0.0625 * (d_k1.T @ xq)
    d_k2 = unpack_weight(d_words, d_scales)[np.arange(K)[:, None], runs(k2, K)]
    x_two = unpack_weight(x_words, x_scales)[:, unstriped(two)]
    b = 0.0625 * (d_k2.T @ x_two)
    z = f64(gn) * (np.maximum(a[np.arange(H)[:, None], runs(n1, H)] + b[np.arange(H)[:, None], runs(n3, H)], a[np.arange(H)[:, None], runs(n2, H)] + b[np.arange(H)[:, None], runs(n4, H)]))
    h = mxq(f64(w1), 0, "e4m3").T @ mxq(z, 0, "e4m3")
    pa = h[np.arange(N)[:, None], runs(n5, N)]
    pb = h[np.arange(N)[:, None], runs(n6, N)]
    rb = pa - pb
    ra = 0.75 * (pa + pb)
    ds = np.zeros((N, S))
    ds[np.arange(N)[:, None], runs(n5, N)] = ra
    out = ds.copy()
    out[np.arange(N)[:, None], runs(n6, N)] = rb
    return out

@@ -1,0 +1,241 @@
+from contextlib import ExitStack
+
+import concourse.mybir as mybir
+
+K, T, S, N, G, H, W = 512, 1024, 512, 512, 2048, 512, 256
+FLOPS = 2 * (K * H * S + K * H * S + H * N * S)
+
+F32 = mybir.dt.float32
+BF16 = mybir.dt.bfloat16
+I32 = mybir.dt.int32
+U32 = mybir.dt.uint32
+U16 = mybir.dt.uint16
+U8 = mybir.dt.uint8
+FP8X4 = mybir.dt.float8_e4m3fn_x4
+COPY = mybir.ActivationFunctionType.Copy
+ADD = mybir.AluOpType.add
+MULT = mybir.AluOpType.mult
+MAX = mybir.AluOpType.max
+
+P = 128
+PACK = 4
+BLOCKS = 16
+CHUNKS = [(0, 256), (256, 256)]
+BOTH_ON_SCALAR = 2
+
+
+def tile_picked_twpqpathbhaar_none_p_kernel(
+    tc, x_words, x_scales, d_words, d_scales, gn, w1, offs, k1, two, k2, n1, n2, n3, n4, n5, n6, out
+):
+    nc = tc.nc
+    with ExitStack() as ctx:
+        held = ctx.enter_context(tc.tile_pool(name="held", bufs=1))
+        picked = ctx.enter_context(tc.tile_pool(name="picked", bufs=1))
+        work = ctx.enter_context(tc.tile_pool(name="work", bufs=1))
+        stage = ctx.enter_context(tc.tile_pool(name="stage", bufs=1))
+        psum = ctx.enter_context(tc.psum_pool(name="psum", bufs=8))
+
+        lists = {}
+
+        def load_list(name, src):
+            lists[name] = held.tile(list(src.shape), U16, name="list_" + name)
+            nc.sync.dma_start(lists[name][:], src)
+
+        def load_scale_rows(name, src, cols):
+            tile = held.tile([P, cols], U8, name=name, align_bytes=64)
+            rows = src[0].bitcast(I32).unsqueeze(1).broadcast_to([BLOCKS, P // BLOCKS, cols // 4])
+            nc.sync.dma_start(tile[:].bitcast(I32), rows)
+            return tile
+
+        def load_words(name, src, cols):
+            tile = held.tile([P, cols], I32, name=name, align_bytes=64)
+            nc.sync.dma_start(tile[:], src[0].rearrange("p c r -> p (c r)").bitcast(I32))
+            return tile
+
+        load_list("k1", k1)
+        d_bytes = load_scale_rows("d_bytes", d_scales, G)
+        load_list("offs", offs)
+        x_bytes = load_scale_rows("x_bytes", x_scales, T)
+        x_tab = load_words("x_tab", x_words, T)
+        d_tab = load_words("d_tab", d_words, G)
+        load_list("k2", k2)
+        load_list("two", two)
+        load_list("n1", n1)
+        load_list("n2", n2)
+        gain = held.tile([P, PACK], F32)
+        nc.sync.dma_start(gain[:], gn.rearrange("(p t) o -> p (t o)", t=PACK))
+        w_raw = []
+        for half in range(2):
+            w_raw.append(stage.tile([P, PACK, N // 2], F32, name="w_raw%d" % half, offset=half * 4096))
+            nc.sync.dma_start(
+                w_raw[half][:], w1.rearrange("(p j) n -> p j n", j=PACK)[:, :, half * N // 2 : (half + 1) * N // 2]
+            )
+        load_list("n3", n3)
+        load_list("n4", n4)
+        load_list("n5", n5)
+        load_list("n6", n6)
+
+        gain16 = held.tile([P, PACK], F32)
+        nc.scalar.activation(gain16[:], gain[:], COPY, scale=0.0625)
+
+        def coded_product(side, code_list, token_list, offsets, queue):
+            d_b = picked.tile([P, H], U8, name="d_b" + side, align_bytes=64, offset=offsets[0])
+            x_b = picked.tile([P, S], U8, name="x_b" + side, align_bytes=64, offset=offsets[1])
+            x_w = picked.tile([P, S], U32, name="x_w" + side, align_bytes=64, offset=offsets[2])
+            d_w = picked.tile([P, H], U32, name="d_w" + side, align_bytes=64, offset=offsets[3])
+            planes = work.tile([P, H + S], U8, name="planes" + side, align_bytes=64)
+            dealt = work.tile([P, H], U32, name="dealt" + side, align_bytes=64)
+            nc.vector.tensor_copy(d_b[:], d_bytes[:].indirect(lists[code_list][:]))
+            nc.vector.tensor_copy(x_b[:], x_bytes[:].indirect(lists[token_list][:]))
+            nc.vector.tensor_copy(
+                planes[:, 0:H].rearrange("p (t m) -> p m t", t=PACK), d_b[:].rearrange("p (m t) -> p m t", t=PACK)
+            )
+            nc.vector.tensor_copy(planes[:, H : H + S].bitcast(I32), x_b[:].bitcast(I32))
+            for c in range(1, 4):
+                queue.dma_start(planes[c:P:32, :].bitcast(I32), planes[8 * c : P : 32, :].bitcast(I32))
+            nc.vector.tensor_copy(x_w[:], x_tab[:].bitcast(U32).indirect(lists[token_list][:]))
+            nc.vector.tensor_copy(d_w[:], d_tab[:].bitcast(U32).indirect(lists[code_list][:]))
+            nc.vector.tensor_copy(
+                dealt[:].rearrange("p (t m) -> p m t", t=PACK), d_w[:].rearrange("p (m t) -> p m t", t=PACK)
+            )
+            banks = []
+            for t in range(PACK):
+                bank = psum.tile([P, S], F32, name="bank", tag="bank")
+                cols = slice(t * P, (t + 1) * P)
+                nc.tensor.matmul_mx(
+                    out=bank[:],
+                    lhsT=dealt[:, cols].bitcast(FP8X4),
+                    lhsT_scale=planes[:, cols],
+                    rhs=x_w[:].bitcast(FP8X4),
+                    rhs_scale=planes[:, H : H + S],
+                    start=True,
+                    stop=True,
+                )
+                banks.append(bank)
+            return banks
+
+        def leave_psum(side, banks, t):
+            if side == "a":
+                tile = stage.tile([P, S], F32, name="rows_a%d" % t, offset=(PACK - 1 - t) * 2048)
+            else:
+                tile = work.tile([P, S], F32, name="rows_b%d" % t)
+            nc.scalar.copy(tile[:], banks[t][:])
+            return tile
+
+        a_banks = coded_product("a", "k1", "offs", (0, 512, 1024, 4608), nc.scalar)
+        b_banks = coded_product("b", "k2", "two", (5120, 5632, 6144, 3072), nc.sync)
+
+        w_grouped = work.tile([P, PACK * N], BF16, align_bytes=64)
+        for half in range(2):
+            nc.scalar.copy(
+                w_grouped[:].rearrange("p (t m j) -> p m j t", t=PACK, j=PACK)[:, half * 64 : (half + 1) * 64],
+                w_raw[half][:].rearrange("p j (m t) -> p m j t", t=PACK),
+            )
+        w_codes = work.tile([P, N], U32, align_bytes=64)
+        w_scales = work.tile([P, N], U8, align_bytes=64)
+        nc.vector.quantize_mx(w_codes[:].bitcast(FP8X4), w_scales[:], w_grouped[:])
+
+        a_rows = [leave_psum("a", a_banks, t) for t in range(PACK)]
+
+        pairs = (("n1", "n3"), ("n2", "n4"))
+
+        def entries(name, c0, cw):
+            return lists[name][:, c0 // 16 : (c0 + cw) // 16]
+
+        a_picked = {}
+
+        def pick_a(c, t):
+            c0, cw = CHUNKS[c]
+            for e in range(2):
+                tile = work.tile([P, cw], F32, name="a_pick%d%d%d" % (c, t, e))
+                nc.scalar.activation(tile[:], a_rows[t][:].indirect(entries(pairs[e][0], c0, cw)), COPY)
+                a_picked[c, t, e] = tile
+
+        for t in range(PACK - 1):
+            pick_a(0, t)
+        b_rows = [leave_psum("b", b_banks, t) for t in range(2)]
+        pick_a(0, PACK - 1)
+        b_rows.extend(leave_psum("b", b_banks, t) for t in range(2, PACK))
+
+        for c in range(1, len(CHUNKS)):
+            for t in range(PACK):
+                pick_a(c, t)
+
+        z_codes = work.tile([P, S], U32, align_bytes=64)
+        z_scales = work.tile([P, S], U8, align_bytes=64)
+        h_rows = [work.tile([P, S], F32, name="h_rows%d" % t) for t in range(PACK)]
+        last_banks = []
+        for c, (c0, cw) in enumerate(CHUNKS):
+            larger = work.tile([P, PACK, cw], F32, name="larger%d" % c)
+            for t in range(PACK):
+                sums = []
+                for e in range(2):
+                    tile = work.tile([P, cw], F32, name="sum%d%d%d" % (c, t, e))
+                    window = b_rows[t][:].indirect(entries(pairs[e][1], c0, cw))
+                    if c == len(CHUNKS) - 1 and t >= PACK - BOTH_ON_SCALAR:
+                        b_pick = work.tile([P, cw], F32, name="b_pick%d%d%d" % (c, t, e))
+                        nc.scalar.activation(b_pick[:], window, COPY)
+                        nc.vector.tensor_tensor(tile[:], b_pick[:], a_picked[c, t, e][:], ADD)
+                    else:
+                        nc.vector.tensor_tensor(tile[:], window, a_picked[c, t, e][:], ADD)
+                    sums.append(tile)
+                nc.vector.tensor_tensor(larger[:, t, :], sums[0][:], sums[1][:], MAX)
+            z_grouped = work.tile([P, cw, PACK], BF16, name="z_grouped%d" % c, align_bytes=64)
+            nc.vector.tensor_tensor(
+                z_grouped[:],
+                larger[:].rearrange("p t c -> p c t"),
+                gain16[:].unsqueeze(1).broadcast_to([P, cw, PACK]),
+                MULT,
+            )
+            cols = slice(c0, c0 + cw)
+            nc.vector.quantize_mx(
+                z_codes[:, cols].bitcast(FP8X4), z_scales[:, cols], z_grouped[:].rearrange("p c t -> p (c t)")
+            )
+            for t in range(PACK):
+                bank = psum.tile([P, S], F32, name="bank", tag="bank")
+                rows = slice(t * P, (t + 1) * P)
+                nc.tensor.matmul_mx(
+                    out=bank[:, 0:cw],
+                    lhsT=w_codes[:, rows].bitcast(FP8X4),
+                    lhsT_scale=w_scales[:, rows],
+                    rhs=z_codes[:, cols].bitcast(FP8X4),
+                    rhs_scale=z_scales[:, cols],
+                    start=True,
+                    stop=True,
+                )
+                if c < len(CHUNKS) - 1:
+                    nc.scalar.copy(h_rows[t][:, cols], bank[:, 0:cw])
+                else:
+                    last_banks.append(bank)
+
+        out_rows = out.rearrange("(p t) n -> p t n", t=PACK)
+        c0, cw = CHUNKS[-1]
+        pa, pb_neg, placed = {}, {}, {}
+
+        def differences(t):
+            nc.scalar.copy(h_rows[t][:, c0 : c0 + cw], last_banks[t][:, 0:cw])
+            pa[t] = work.tile([P, W], F32, name="pa%d" % t)
+            pb_neg[t] = work.tile([P, W], F32, name="pb_neg%d" % t)
+            nc.scalar.activation(pa[t][:], h_rows[t][:].indirect(lists["n5"][:]), COPY)
+            if t == 0:
+                nc.vector.tensor_scalar(pb_neg[t][:], h_rows[t][:].indirect(lists["n6"][:]), -1.0, 0.0, MULT, ADD)
+            else:
+                nc.scalar.activation(pb_neg[t][:], h_rows[t][:].indirect(lists["n6"][:]), COPY, scale=-1.0)
+            placed[t] = work.tile([P, S], F32, name="placed%d" % t)
+            nc.vector.tensor_tensor(placed[t][:].indirect(lists["n6"][:]), pa[t][:], pb_neg[t][:], ADD)
+
+        def sums_out(t):
+            qa = work.tile([P, W], F32, name="qa%d" % t)
+            qb = work.tile([P, W], F32, name="qb%d" % t)
+            nc.scalar.activation(qa[:], pa[t][:], COPY, scale=0.75)
+            nc.scalar.activation(qb[:], pb_neg[t][:], COPY, scale=-0.75)
+            nc.vector.tensor_tensor(placed[t][:].indirect(lists["n5"][:]), qa[:], qb[:], ADD)
+            nc.sync.dma_start(out_rows[:, t, :], placed[t][:])
+
+        differences(0)
+        sums_out(0)
+        differences(1)
+        for t in range(1, PACK):
+            if t + 1 < PACK:
+                differences(t + 1)
+            sums_out(t)

@@ -21,7 +21,7 @@ P = 128
 PACK = 4
 BLOCKS = 16
 CHUNKS = [(0, 256), (256, 256)]
-BOTH_ON_SCALAR = 2
+BOTH_ON_SCALAR = 3
 
 
 def tile_picked_twpqpathbhaar_none_p_kernel(
@@ -32,7 +32,6 @@ def tile_picked_twpqpathbhaar_none_p_kernel(
         held = ctx.enter_context(tc.tile_pool(name="held", bufs=1))
         picked = ctx.enter_context(tc.tile_pool(name="picked", bufs=1))
         work = ctx.enter_context(tc.tile_pool(name="work", bufs=1))
-        stage = ctx.enter_context(tc.tile_pool(name="stage", bufs=1))
         psum = ctx.enter_context(tc.psum_pool(name="psum", bufs=8))
 
         lists = {}
@@ -55,22 +54,21 @@ def tile_picked_twpqpathbhaar_none_p_kernel(
         load_list("k1", k1)
         d_bytes = load_scale_rows("d_bytes", d_scales, G)
         load_list("offs", offs)
-        x_bytes = load_scale_rows("x_bytes", x_scales, T)
+        x_bytes = held.tile([P, T], U8, align_bytes=64)
+        for r in range(4):
+            rows = x_scales[0].bitcast(I32)[r:BLOCKS:4, :].unsqueeze(1).broadcast_to([4, 8, T // 4])
+            nc.sync.dma_start(x_bytes[r:P:4, :].bitcast(I32), rows)
         x_tab = load_words("x_tab", x_words, T)
         d_tab = load_words("d_tab", d_words, G)
         load_list("k2", k2)
         load_list("two", two)
-        load_list("n1", n1)
-        load_list("n2", n2)
         gain = held.tile([P, PACK], F32)
         nc.sync.dma_start(gain[:], gn.rearrange("(p t) o -> p (t o)", t=PACK))
-        w_raw = []
-        for half in range(2):
-            w_raw.append(stage.tile([P, PACK, N // 2], F32, name="w_raw%d" % half, offset=half * 4096))
-            nc.sync.dma_start(
-                w_raw[half][:], w1.rearrange("(p j) n -> p j n", j=PACK)[:, :, half * N // 2 : (half + 1) * N // 2]
-            )
+        load_list("n1", n1)
+        load_list("n2", n2)
         load_list("n3", n3)
+        w_raw = held.tile([P, PACK, N], F32)
+        nc.sync.dma_start(w_raw[:], w1.rearrange("(p j) n -> p j n", j=PACK))
         load_list("n4", n4)
         load_list("n5", n5)
         load_list("n6", n6)
@@ -83,16 +81,15 @@ def tile_picked_twpqpathbhaar_none_p_kernel(
             x_b = picked.tile([P, S], U8, name="x_b" + side, align_bytes=64, offset=offsets[1])
             x_w = picked.tile([P, S], U32, name="x_w" + side, align_bytes=64, offset=offsets[2])
             d_w = picked.tile([P, H], U32, name="d_w" + side, align_bytes=64, offset=offsets[3])
-            planes = work.tile([P, H + S], U8, name="planes" + side, align_bytes=64)
+            planes = work.tile([P, H], U8, name="planes" + side, align_bytes=64)
             dealt = work.tile([P, H], U32, name="dealt" + side, align_bytes=64)
             nc.vector.tensor_copy(d_b[:], d_bytes[:].indirect(lists[code_list][:]))
-            nc.vector.tensor_copy(x_b[:], x_bytes[:].indirect(lists[token_list][:]))
             nc.vector.tensor_copy(
                 planes[:, 0:H].rearrange("p (t m) -> p m t", t=PACK), d_b[:].rearrange("p (m t) -> p m t", t=PACK)
             )
-            nc.vector.tensor_copy(planes[:, H : H + S].bitcast(I32), x_b[:].bitcast(I32))
             for c in range(1, 4):
                 queue.dma_start(planes[c:P:32, :].bitcast(I32), planes[8 * c : P : 32, :].bitcast(I32))
+            nc.vector.tensor_copy(x_b[:], x_bytes[:].indirect(lists[token_list][:]))
             nc.vector.tensor_copy(x_w[:], x_tab[:].bitcast(U32).indirect(lists[token_list][:]))
             nc.vector.tensor_copy(d_w[:], d_tab[:].bitcast(U32).indirect(lists[code_list][:]))
             nc.vector.tensor_copy(
@@ -107,7 +104,7 @@ def tile_picked_twpqpathbhaar_none_p_kernel(
                     lhsT=dealt[:, cols].bitcast(FP8X4),
                     lhsT_scale=planes[:, cols],
                     rhs=x_w[:].bitcast(FP8X4),
-                    rhs_scale=planes[:, H : H + S],
+                    rhs_scale=x_b[:],
                     start=True,
                     stop=True,
                 )
@@ -115,27 +112,15 @@ def tile_picked_twpqpathbhaar_none_p_kernel(
             return banks
 
         def leave_psum(side, banks, t):
-            if side == "a":
-                tile = stage.tile([P, S], F32, name="rows_a%d" % t, offset=(PACK - 1 - t) * 2048)
-            else:
-                tile = work.tile([P, S], F32, name="rows_b%d" % t)
+            tile = work.tile([P, S], F32, name="rows_%s%d" % (side, t))
             nc.scalar.copy(tile[:], banks[t][:])
             return tile
 
         a_banks = coded_product("a", "k1", "offs", (0, 512, 1024, 4608), nc.scalar)
         b_banks = coded_product("b", "k2", "two", (5120, 5632, 6144, 3072), nc.sync)
 
-        w_grouped = work.tile([P, PACK * N], BF16, align_bytes=64)
-        for half in range(2):
-            nc.scalar.copy(
-                w_grouped[:].rearrange("p (t m j) -> p m j t", t=PACK, j=PACK)[:, half * 64 : (half + 1) * 64],
-                w_raw[half][:].rearrange("p j (m t) -> p m j t", t=PACK),
-            )
-        w_codes = work.tile([P, N], U32, align_bytes=64)
-        w_scales = work.tile([P, N], U8, align_bytes=64)
-        nc.vector.quantize_mx(w_codes[:].bitcast(FP8X4), w_scales[:], w_grouped[:])
-
         a_rows = [leave_psum("a", a_banks, t) for t in range(PACK)]
+
 
         pairs = (("n1", "n3"), ("n2", "n4"))
 
@@ -147,73 +132,98 @@ def tile_picked_twpqpathbhaar_none_p_kernel(
         def pick_a(c, t):
             c0, cw = CHUNKS[c]
             for e in range(2):
-                tile = work.tile([P, cw], F32, name="a_pick%d%d%d" % (c, t, e))
-                nc.scalar.activation(tile[:], a_rows[t][:].indirect(entries(pairs[e][0], c0, cw)), COPY)
+                window = a_rows[t][:].indirect(entries(pairs[e][0], c0, cw))
+                if t == PACK - 1:
+                    tile = picked.tile([P, cw], F32, name="a_pick%d%d" % (t, e), offset=3072 + 1024 * e)
+                else:
+                    tile = work.tile([P, cw], F32, name="a_pick%d%d" % (t, e))
+                if c == 0 and t == PACK - 1:
+                    nc.vector.tensor_copy(tile[:], window)
+                else:
+                    nc.scalar.activation(tile[:], window, COPY)
                 a_picked[c, t, e] = tile
 
-        for t in range(PACK - 1):
-            pick_a(0, t)
+        pick_a(0, 3)
+        pick_a(0, 0)
+        pick_a(0, 1)
         b_rows = [leave_psum("b", b_banks, t) for t in range(2)]
-        pick_a(0, PACK - 1)
+        pick_a(0, 2)
         b_rows.extend(leave_psum("b", b_banks, t) for t in range(2, PACK))
 
-        for c in range(1, len(CHUNKS)):
-            for t in range(PACK):
-                pick_a(c, t)
+        w_grouped = picked.tile([P, PACK * N], BF16, align_bytes=64, offset=6144)
+        nc.scalar.copy(
+            w_grouped[:].rearrange("p (t m j) -> p m j t", t=PACK, j=PACK),
+            w_raw[:].rearrange("p j (m t) -> p m j t", t=PACK),
+        )
+        w_codes = {0: work.tile([P, P], U32, name="w_codes0", align_bytes=64)}
+        w_scales = work.tile([P, P], U8, align_bytes=64)
+        w_planes = {0: w_scales}
 
         z_codes = work.tile([P, S], U32, align_bytes=64)
         z_scales = work.tile([P, S], U8, align_bytes=64)
         h_rows = [work.tile([P, S], F32, name="h_rows%d" % t) for t in range(PACK)]
-        last_banks = []
+
+        def dense(t, cols):
+            bank = psum.tile([P, cols.stop - cols.start], F32, name="bank", tag="bank")
+            nc.tensor.matmul_mx(
+                out=bank[:],
+                lhsT=w_codes[t][:, 0:P].bitcast(FP8X4),
+                lhsT_scale=w_planes[t][:, 0:P],
+                rhs=z_codes[:, cols].bitcast(FP8X4),
+                rhs_scale=z_scales[:, cols],
+                start=True,
+                stop=True,
+            )
+            return bank
+
         for c, (c0, cw) in enumerate(CHUNKS):
+            cols = slice(c0, c0 + cw)
             larger = work.tile([P, PACK, cw], F32, name="larger%d" % c)
-            for t in range(PACK):
-                sums = []
-                for e in range(2):
-                    tile = work.tile([P, cw], F32, name="sum%d%d%d" % (c, t, e))
-                    window = b_rows[t][:].indirect(entries(pairs[e][1], c0, cw))
-                    if c == len(CHUNKS) - 1 and t >= PACK - BOTH_ON_SCALAR:
-                        b_pick = work.tile([P, cw], F32, name="b_pick%d%d%d" % (c, t, e))
-                        nc.scalar.activation(b_pick[:], window, COPY)
-                        nc.vector.tensor_tensor(tile[:], b_pick[:], a_picked[c, t, e][:], ADD)
-                    else:
-                        nc.vector.tensor_tensor(tile[:], window, a_picked[c, t, e][:], ADD)
-                    sums.append(tile)
-                nc.vector.tensor_tensor(larger[:, t, :], sums[0][:], sums[1][:], MAX)
-            z_grouped = work.tile([P, cw, PACK], BF16, name="z_grouped%d" % c, align_bytes=64)
+            for pair in range(2):
+                sums = work.tile([P, 2, 2, cw], F32, name="sums%d%d" % (c, pair))
+                for t in range(2 * pair, 2 * pair + 2):
+                    if c > 0:
+                        pick_a(c, t)
+                    for e in range(2):
+                        window = b_rows[t][:].indirect(entries(pairs[e][1], c0, cw))
+                        if c == len(CHUNKS) - 1 and 2 * t + e >= 2 * PACK - BOTH_ON_SCALAR:
+                            b_pick = work.tile([P, cw], F32, name="b_pick%d%d%d" % (c, t, e))
+                            nc.scalar.activation(b_pick[:], window, COPY)
+                            nc.vector.tensor_tensor(sums[:, e, t % 2, :], b_pick[:], a_picked[c, t, e][:], ADD)
+                        else:
+                            nc.vector.tensor_tensor(sums[:, e, t % 2, :], window, a_picked[c, t, e][:], ADD)
+                    if c == len(CHUNKS) - 1 and pair == 1:
+                        nc.vector.tensor_tensor(larger[:, t, :], sums[:, 0, t % 2], sums[:, 1, t % 2], MAX)
+                if c < len(CHUNKS) - 1 or pair == 0:
+                    nc.vector.tensor_tensor(larger[:, 2 * pair : 2 * pair + 2, :], sums[:, 0], sums[:, 1], MAX)
+            z_grouped = work.tile([P, cw, PACK], BF16, name="z_grouped%d" % c, tag="z_grouped%d" % c, align_bytes=64)
             nc.vector.tensor_tensor(
                 z_grouped[:],
                 larger[:].rearrange("p t c -> p c t"),
                 gain16[:].unsqueeze(1).broadcast_to([P, cw, PACK]),
                 MULT,
             )
-            cols = slice(c0, c0 + cw)
+            if c == 0:
+                nc.vector.quantize_mx(w_codes[0][:].bitcast(FP8X4), w_scales[:, 0:P], w_grouped[:, 0 : PACK * P])
             nc.vector.quantize_mx(
                 z_codes[:, cols].bitcast(FP8X4), z_scales[:, cols], z_grouped[:].rearrange("p c t -> p (c t)")
             )
-            for t in range(PACK):
-                bank = psum.tile([P, S], F32, name="bank", tag="bank")
-                rows = slice(t * P, (t + 1) * P)
-                nc.tensor.matmul_mx(
-                    out=bank[:, 0:cw],
-                    lhsT=w_codes[:, rows].bitcast(FP8X4),
-                    lhsT_scale=w_scales[:, rows],
-                    rhs=z_codes[:, cols].bitcast(FP8X4),
-                    rhs_scale=z_scales[:, cols],
-                    start=True,
-                    stop=True,
-                )
-                if c < len(CHUNKS) - 1:
-                    nc.scalar.copy(h_rows[t][:, cols], bank[:, 0:cw])
-                else:
-                    last_banks.append(bank)
+            bank = dense(0, cols)
+            nc.scalar.copy(h_rows[0][:, cols], bank[:])
+        w_rest = work.tile([P, N - P], U32, tag="z_grouped%d" % (len(CHUNKS) - 1), align_bytes=64)
+        w_rest_scales = work.tile([P, N - P], U8, align_bytes=64)
+        nc.vector.quantize_mx(w_rest[:].bitcast(FP8X4), w_rest_scales[:], w_grouped[:, PACK * P :])
+        for t in range(1, PACK):
+            w_codes[t] = w_rest[:, (t - 1) * P : t * P]
+            w_planes[t] = w_rest_scales[:, (t - 1) * P : t * P]
+        last_banks = {t: dense(t, slice(0, S)) for t in range(1, PACK)}
 
         out_rows = out.rearrange("(p t) n -> p t n", t=PACK)
-        c0, cw = CHUNKS[-1]
         pa, pb_neg, placed = {}, {}, {}
 
         def differences(t):
-            nc.scalar.copy(h_rows[t][:, c0 : c0 + cw], last_banks[t][:, 0:cw])
+            if t > 0:
+                nc.scalar.copy(h_rows[t][:], last_banks[t][:])
             pa[t] = work.tile([P, W], F32, name="pa%d" % t)
             pb_neg[t] = work.tile([P, W], F32, name="pb_neg%d" % t)
             nc.scalar.activation(pa[t][:], h_rows[t][:].indirect(lists["n5"][:]), COPY)
@@ -230,7 +240,11 @@ def tile_picked_twpqpathbhaar_none_p_kernel(
             nc.scalar.activation(qa[:], pa[t][:], COPY, scale=0.75)
             nc.scalar.activation(qb[:], pb_neg[t][:], COPY, scale=-0.75)
             nc.vector.tensor_tensor(placed[t][:].indirect(lists["n5"][:]), qa[:], qb[:], ADD)
-            nc.sync.dma_start(out_rows[:, t, :], placed[t][:])
+            if t < PACK - 1:
+                nc.sync.dma_start(out_rows[:, t, :], placed[t][:])
+            else:
+                nc.sync.dma_start(out_rows[:, t, 0:W], placed[t][:, 0:W])
+                nc.scalar.dma_start(out_rows[:, t, W:S], placed[t][:, W:S])
 
         differences(0)
         sums_out(0)

@@ -21,7 +21,7 @@ P = 128
 PACK = 4
 BLOCKS = 16
 CHUNKS = [(0, 256), (256, 256)]
-BOTH_ON_SCALAR = 3
+BOTH_ON_SCALAR = 6
 
 
 def tile_picked_twpqpathbhaar_none_p_kernel(
@@ -55,9 +55,9 @@ def tile_picked_twpqpathbhaar_none_p_kernel(
         d_bytes = load_scale_rows("d_bytes", d_scales, G)
         load_list("offs", offs)
         x_bytes = held.tile([P, T], U8, align_bytes=64)
-        for r in range(4):
-            rows = x_scales[0].bitcast(I32)[r:BLOCKS:4, :].unsqueeze(1).broadcast_to([4, 8, T // 4])
-            nc.sync.dma_start(x_bytes[r:P:4, :].bitcast(I32), rows)
+        for q in range(4):
+            rows = x_scales[0].bitcast(I32)[4 * q : 4 * q + 4, :].unsqueeze(0).broadcast_to([8, 4, T // 4])
+            nc.sync.dma_start(x_bytes[32 * q : 32 * q + 32, :].bitcast(I32), rows)
         x_tab = load_words("x_tab", x_words, T)
         d_tab = load_words("d_tab", d_words, G)
         load_list("k2", k2)
@@ -85,7 +85,7 @@ def tile_picked_twpqpathbhaar_none_p_kernel(
             dealt = work.tile([P, H], U32, name="dealt" + side, align_bytes=64)
             nc.vector.tensor_copy(d_b[:], d_bytes[:].indirect(lists[code_list][:]))
             nc.vector.tensor_copy(
-                planes[:, 0:H].rearrange("p (t m) -> p m t", t=PACK), d_b[:].rearrange("p (m t) -> p m t", t=PACK)
+                planes[:].rearrange("p (t m) -> p t m", t=PACK), d_b[:].rearrange("p (m t) -> p t m", t=PACK)
             )
             for c in range(1, 4):
                 queue.dma_start(planes[c:P:32, :].bitcast(I32), planes[8 * c : P : 32, :].bitcast(I32))
@@ -129,25 +129,25 @@ def tile_picked_twpqpathbhaar_none_p_kernel(
 
         a_picked = {}
 
-        def pick_a(c, t):
+        def pick_a(c, t, e):
             c0, cw = CHUNKS[c]
-            for e in range(2):
-                window = a_rows[t][:].indirect(entries(pairs[e][0], c0, cw))
-                if t == PACK - 1:
-                    tile = picked.tile([P, cw], F32, name="a_pick%d%d" % (t, e), offset=3072 + 1024 * e)
-                else:
-                    tile = work.tile([P, cw], F32, name="a_pick%d%d" % (t, e))
-                if c == 0 and t == PACK - 1:
-                    nc.vector.tensor_copy(tile[:], window)
-                else:
-                    nc.scalar.activation(tile[:], window, COPY)
-                a_picked[c, t, e] = tile
+            window = a_rows[t][:].indirect(entries(pairs[e][0], c0, cw))
+            if t == PACK - 1:
+                tile = picked.tile([P, cw], F32, name="a_pick%d%d" % (t, e), offset=3072 + 1024 * e)
+            else:
+                tile = work.tile([P, cw], F32, name="a_pick%d%d" % (t, e))
+            if c == 0 and t == PACK - 1:
+                nc.vector.tensor_copy(tile[:], window)
+            else:
+                nc.scalar.activation(tile[:], window, COPY)
+            a_picked[c, t, e] = tile
 
-        pick_a(0, 3)
-        pick_a(0, 0)
-        pick_a(0, 1)
+        for t in (3, 0, 1):
+            for e in range(2):
+                pick_a(0, t, e)
         b_rows = [leave_psum("b", b_banks, t) for t in range(2)]
-        pick_a(0, 2)
+        for e in range(2):
+            pick_a(0, 2, e)
         b_rows.extend(leave_psum("b", b_banks, t) for t in range(2, PACK))
 
         w_grouped = picked.tile([P, PACK * N], BF16, align_bytes=64, offset=6144)
@@ -177,37 +177,43 @@ def tile_picked_twpqpathbhaar_none_p_kernel(
             return bank
 
         for c, (c0, cw) in enumerate(CHUNKS):
-            cols = slice(c0, c0 + cw)
+            last = c == len(CHUNKS) - 1
+            halves = [slice(0, cw // 2), slice(cw // 2, cw)]
+            sums = work.tile([P, 2, PACK, cw], F32, name="sums%d" % c)
             larger = work.tile([P, PACK, cw], F32, name="larger%d" % c)
-            for pair in range(2):
-                sums = work.tile([P, 2, 2, cw], F32, name="sums%d%d" % (c, pair))
-                for t in range(2 * pair, 2 * pair + 2):
+            for t in range(PACK):
+                for e in range(2):
                     if c > 0:
-                        pick_a(c, t)
-                    for e in range(2):
-                        window = b_rows[t][:].indirect(entries(pairs[e][1], c0, cw))
-                        if c == len(CHUNKS) - 1 and 2 * t + e >= 2 * PACK - BOTH_ON_SCALAR:
-                            b_pick = work.tile([P, cw], F32, name="b_pick%d%d%d" % (c, t, e))
-                            nc.scalar.activation(b_pick[:], window, COPY)
-                            nc.vector.tensor_tensor(sums[:, e, t % 2, :], b_pick[:], a_picked[c, t, e][:], ADD)
-                        else:
-                            nc.vector.tensor_tensor(sums[:, e, t % 2, :], window, a_picked[c, t, e][:], ADD)
-                    if c == len(CHUNKS) - 1 and pair == 1:
-                        nc.vector.tensor_tensor(larger[:, t, :], sums[:, 0, t % 2], sums[:, 1, t % 2], MAX)
-                if c < len(CHUNKS) - 1 or pair == 0:
-                    nc.vector.tensor_tensor(larger[:, 2 * pair : 2 * pair + 2, :], sums[:, 0], sums[:, 1], MAX)
+                        pick_a(c, t, e)
+                    window = b_rows[t][:].indirect(entries(pairs[e][1], c0, cw))
+                    if last and 2 * t + e >= 2 * PACK - BOTH_ON_SCALAR:
+                        b_pick = work.tile([P, cw], F32, name="b_pick%d%d" % (t, e))
+                        nc.scalar.activation(b_pick[:], window, COPY)
+                        for part in halves if (t, e) == (PACK - 1, 1) else [slice(0, cw)]:
+                            nc.vector.tensor_tensor(sums[:, e, t, part], b_pick[:, part], a_picked[c, t, e][:, part], ADD)
+                    else:
+                        nc.vector.tensor_tensor(sums[:, e, t, :], window, a_picked[c, t, e][:], ADD)
+                if last and t == PACK - 2:
+                    nc.vector.tensor_tensor(larger[:, 0 : t + 1, :], sums[:, 0, 0 : t + 1, :], sums[:, 1, 0 : t + 1, :], MAX)
+            first = PACK - 1 if last else 0
+            for part in halves:
+                nc.vector.tensor_tensor(larger[:, first:, part], sums[:, 0, first:, part], sums[:, 1, first:, part], MAX)
             z_grouped = work.tile([P, cw, PACK], BF16, name="z_grouped%d" % c, tag="z_grouped%d" % c, align_bytes=64)
-            nc.vector.tensor_tensor(
-                z_grouped[:],
-                larger[:].rearrange("p t c -> p c t"),
-                gain16[:].unsqueeze(1).broadcast_to([P, cw, PACK]),
-                MULT,
-            )
+            for part in halves:
+                nc.vector.tensor_tensor(
+                    z_grouped[:, part, :].rearrange("p (c i) t -> p c t i", i=4),
+                    larger[:, :, part].rearrange("p t (c i) -> p c t i", i=4),
+                    gain16[:].unsqueeze(1).unsqueeze(3).broadcast_to([P, cw // 8, PACK, 4]),
+                    MULT,
+                )
             if c == 0:
                 nc.vector.quantize_mx(w_codes[0][:].bitcast(FP8X4), w_scales[:, 0:P], w_grouped[:, 0 : PACK * P])
-            nc.vector.quantize_mx(
-                z_codes[:, cols].bitcast(FP8X4), z_scales[:, cols], z_grouped[:].rearrange("p c t -> p (c t)")
-            )
+            for part in halves:
+                cols = slice(c0 + part.start, c0 + part.stop)
+                nc.vector.quantize_mx(
+                    z_codes[:, cols].bitcast(FP8X4), z_scales[:, cols], z_grouped[:, part, :].rearrange("p c t -> p (c t)")
+                )
+            cols = slice(c0, c0 + cw)
             bank = dense(0, cols)
             nc.scalar.copy(h_rows[0][:, cols], bank[:])
         w_rest = work.tile([P, N - P], U32, tag="z_grouped%d" % (len(CHUNKS) - 1), align_bytes=64)

@@ -62,19 +62,12 @@ def tile_picked_twpqpathbhaar_none_p_kernel(
         d_tab = load_words("d_tab", d_words, G)
         load_list("k2", k2)
         load_list("two", two)
-        gain = held.tile([P, PACK], F32)
-        nc.sync.dma_start(gain[:], gn.rearrange("(p t) o -> p (t o)", t=PACK))
         load_list("n1", n1)
         load_list("n2", n2)
         load_list("n3", n3)
-        w_raw = held.tile([P, PACK, N], F32)
-        nc.sync.dma_start(w_raw[:], w1.rearrange("(p j) n -> p j n", j=PACK))
         load_list("n4", n4)
         load_list("n5", n5)
         load_list("n6", n6)
-
-        gain16 = held.tile([P, PACK], F32)
-        nc.scalar.activation(gain16[:], gain[:], COPY, scale=0.0625)
 
         def coded_product(side, code_list, token_list, offsets, queue):
             d_b = picked.tile([P, H], U8, name="d_b" + side, align_bytes=64, offset=offsets[0])
@@ -85,7 +78,8 @@ def tile_picked_twpqpathbhaar_none_p_kernel(
             dealt = work.tile([P, H], U32, name="dealt" + side, align_bytes=64)
             nc.vector.tensor_copy(d_b[:], d_bytes[:].indirect(lists[code_list][:]))
             nc.vector.tensor_copy(
-                planes[:].rearrange("p (t m) -> p t m", t=PACK), d_b[:].rearrange("p (m t) -> p t m", t=PACK)
+                planes[:].bitcast(I32).rearrange("p (t b q) -> p t b q", t=PACK, q=2),
+                d_b[:].bitcast(I32).rearrange("p (b t q) -> p t b q", t=PACK, q=2),
             )
             for c in range(1, 4):
                 queue.dma_start(planes[c:P:32, :].bitcast(I32), planes[8 * c : P : 32, :].bitcast(I32))
@@ -93,7 +87,8 @@ def tile_picked_twpqpathbhaar_none_p_kernel(
             nc.vector.tensor_copy(x_w[:], x_tab[:].bitcast(U32).indirect(lists[token_list][:]))
             nc.vector.tensor_copy(d_w[:], d_tab[:].bitcast(U32).indirect(lists[code_list][:]))
             nc.vector.tensor_copy(
-                dealt[:].rearrange("p (t m) -> p m t", t=PACK), d_w[:].rearrange("p (m t) -> p m t", t=PACK)
+                dealt[:].rearrange("p (t b q) -> p t b q", t=PACK, q=8),
+                d_w[:].rearrange("p (b t q) -> p t b q", t=PACK, q=8),
             )
             banks = []
             for t in range(PACK):
@@ -112,12 +107,20 @@ def tile_picked_twpqpathbhaar_none_p_kernel(
             return banks
 
         def leave_psum(side, banks, t):
-            tile = work.tile([P, S], F32, name="rows_%s%d" % (side, t))
-            nc.scalar.copy(tile[:], banks[t][:])
+            tile = work.tile([P, S], F32, name="rows_%s%d" % (side, t), tag="rows_%s%d" % (side, t), align_bytes=64)
+            nc.scalar.activation(tile[:], banks[t][:], COPY, scale=0.0625)
             return tile
 
-        a_banks = coded_product("a", "k1", "offs", (0, 512, 1024, 4608), nc.scalar)
+        a_banks = coded_product("a", "k1", "offs", (0, 512, 8192, 4608), nc.scalar)
         b_banks = coded_product("b", "k2", "two", (5120, 5632, 6144, 3072), nc.sync)
+
+        w_raw = picked.tile([P, PACK, N], F32, align_bytes=64, offset=8192)
+        for j in range(PACK):
+            nc.sync.dma_start(w_raw[:, j, :], w1.rearrange("(b t q) n -> t b q n", t=PACK, q=8)[j])
+        gain = picked.tile([P, PACK, 8], F32, align_bytes=64, offset=512)
+        for t in range(PACK):
+            with nc.allow_non_contiguous_dma(reason="one gain a partition"):
+                nc.sync.dma_start(gain[:, t, 0:1], gn.rearrange("(b t q) o -> t b q o", t=PACK, q=8)[t])
 
         a_rows = [leave_psum("a", a_banks, t) for t in range(PACK)]
 
@@ -150,11 +153,9 @@ def tile_picked_twpqpathbhaar_none_p_kernel(
             pick_a(0, 2, e)
         b_rows.extend(leave_psum("b", b_banks, t) for t in range(2, PACK))
 
-        w_grouped = picked.tile([P, PACK * N], BF16, align_bytes=64, offset=6144)
-        nc.scalar.copy(
-            w_grouped[:].rearrange("p (t m j) -> p m j t", t=PACK, j=PACK),
-            w_raw[:].rearrange("p j (m t) -> p m j t", t=PACK),
-        )
+        w_by_tile = w_raw[:].rearrange("p j (b t q) -> p t b q j", t=PACK, q=8)
+        w_grouped = picked.tile([P, PACK * P], BF16, align_bytes=64, offset=6144)
+        nc.scalar.copy(w_grouped[:].rearrange("p (b q j) -> p b q j", q=8, j=PACK), w_by_tile[:, 0])
         w_codes = {0: work.tile([P, P], U32, name="w_codes0", align_bytes=64)}
         w_scales = work.tile([P, P], U8, align_bytes=64)
         w_planes = {0: w_scales}
@@ -176,6 +177,7 @@ def tile_picked_twpqpathbhaar_none_p_kernel(
             )
             return bank
 
+        first_banks = []
         for c, (c0, cw) in enumerate(CHUNKS):
             last = c == len(CHUNKS) - 1
             halves = [slice(0, cw // 2), slice(cw // 2, cw)]
@@ -203,28 +205,36 @@ def tile_picked_twpqpathbhaar_none_p_kernel(
                 nc.vector.tensor_tensor(
                     z_grouped[:, part, :].rearrange("p (c i) t -> p c t i", i=4),
                     larger[:, :, part].rearrange("p t (c i) -> p c t i", i=4),
-                    gain16[:].unsqueeze(1).unsqueeze(3).broadcast_to([P, cw // 8, PACK, 4]),
+                    gain[:, :, 0:1].unsqueeze(1).broadcast_to([P, cw // 8, PACK, 4]),
                     MULT,
                 )
             if c == 0:
-                nc.vector.quantize_mx(w_codes[0][:].bitcast(FP8X4), w_scales[:, 0:P], w_grouped[:, 0 : PACK * P])
+                nc.vector.quantize_mx(w_codes[0][:].bitcast(FP8X4), w_scales[:, 0:P], w_grouped[:])
             for part in halves:
                 cols = slice(c0 + part.start, c0 + part.stop)
                 nc.vector.quantize_mx(
                     z_codes[:, cols].bitcast(FP8X4), z_scales[:, cols], z_grouped[:, part, :].rearrange("p c t -> p (c t)")
                 )
-            cols = slice(c0, c0 + cw)
-            bank = dense(0, cols)
+            for part in halves if last else [slice(0, cw)]:
+                cols = slice(c0 + part.start, c0 + part.stop)
+                first_banks.append((cols, dense(0, cols)))
+            if not last:
+                nc.scalar.copy(h_rows[0][:, cols], first_banks.pop()[1][:])
+        w_rest_grouped = work.tile([P, PACK * (N - P)], BF16, tag="rows_b3", align_bytes=64)
+        nc.scalar.copy(
+            w_rest_grouped[:].rearrange("p (t b q j) -> p t b q j", t=PACK - 1, q=8, j=PACK), w_by_tile[:, 1:PACK]
+        )
+        for cols, bank in first_banks:
             nc.scalar.copy(h_rows[0][:, cols], bank[:])
         w_rest = work.tile([P, N - P], U32, tag="z_grouped%d" % (len(CHUNKS) - 1), align_bytes=64)
         w_rest_scales = work.tile([P, N - P], U8, align_bytes=64)
-        nc.vector.quantize_mx(w_rest[:].bitcast(FP8X4), w_rest_scales[:], w_grouped[:, PACK * P :])
+        nc.vector.quantize_mx(w_rest[:].bitcast(FP8X4), w_rest_scales[:], w_rest_grouped[:])
         for t in range(1, PACK):
             w_codes[t] = w_rest[:, (t - 1) * P : t * P]
             w_planes[t] = w_rest_scales[:, (t - 1) * P : t * P]
         last_banks = {t: dense(t, slice(0, S)) for t in range(1, PACK)}
 
-        out_rows = out.rearrange("(p t) n -> p t n", t=PACK)
+        out_rows = out.rearrange("(b t q) n -> t b q n", t=PACK, q=8)
         pa, pb_neg, placed = {}, {}, {}
 
         def differences(t):
@@ -247,10 +257,10 @@ def tile_picked_twpqpathbhaar_none_p_kernel(
             nc.scalar.activation(qb[:], pb_neg[t][:], COPY, scale=-0.75)
             nc.vector.tensor_tensor(placed[t][:].indirect(lists["n5"][:]), qa[:], qb[:], ADD)
             if t < PACK - 1:
-                nc.sync.dma_start(out_rows[:, t, :], placed[t][:])
+                nc.sync.dma_start(out_rows[t], placed[t][:])
             else:
-                nc.sync.dma_start(out_rows[:, t, 0:W], placed[t][:, 0:W])
-                nc.scalar.dma_start(out_rows[:, t, W:S], placed[t][:, W:S])
+                nc.sync.dma_start(out_rows[t][:, :, 0:W], placed[t][:, 0:W])
+                nc.scalar.dma_start(out_rows[t][:, :, W:S], placed[t][:, W:S])
 
         differences(0)
         sums_out(0)

@@ -18,10 +18,19 @@ MULT = mybir.AluOpType.mult
 MAX = mybir.AluOpType.max
 
 P = 128
-PACK = 4
+TILES = 4
+LAST_TILE = TILES - 1
 BLOCKS = 16
-CHUNKS = [(0, 256), (256, 256)]
-BOTH_ON_SCALAR = 6
+RUN = 8
+QUADRANT = 32
+GROUP = 16
+CHUNK = 256
+HALVES = (slice(0, CHUNK // 2), slice(CHUNK // 2, CHUNK))
+SUM_LISTS = (("n1", "n3"), ("n2", "n4"))
+FUSED_TILES = 1
+
+PLACE_A = {"d_b": 0, "x_b": 512, "x_w": 8320, "d_w": (4096, 6144)}
+PLACE_B = {"d_b": 4160, "x_b": 5696, "x_w": 6208, "d_w": (3136, 4672)}
 
 
 def tile_picked_twpqpathbhaar_none_p_kernel(
@@ -40,64 +49,65 @@ def tile_picked_twpqpathbhaar_none_p_kernel(
             lists[name] = held.tile(list(src.shape), U16, name="list_" + name)
             nc.sync.dma_start(lists[name][:], src)
 
-        def load_scale_rows(name, src, cols):
-            tile = held.tile([P, cols], U8, name=name, align_bytes=64)
-            rows = src[0].bitcast(I32).unsqueeze(1).broadcast_to([BLOCKS, P // BLOCKS, cols // 4])
-            nc.sync.dma_start(tile[:].bitcast(I32), rows)
-            return tile
-
         def load_words(name, src, cols):
             tile = held.tile([P, cols], I32, name=name, align_bytes=64)
             nc.sync.dma_start(tile[:], src[0].rearrange("p c r -> p (c r)").bitcast(I32))
             return tile
 
         load_list("k1", k1)
-        d_bytes = load_scale_rows("d_bytes", d_scales, G)
+        d_bytes = held.tile([P, G], U8, align_bytes=64)
+        nc.sync.dma_start(
+            d_bytes[:].bitcast(I32), d_scales[0].bitcast(I32).unsqueeze(1).broadcast_to([BLOCKS, RUN, G // 4])
+        )
         load_list("offs", offs)
         x_bytes = held.tile([P, T], U8, align_bytes=64)
-        for q in range(4):
-            rows = x_scales[0].bitcast(I32)[4 * q : 4 * q + 4, :].unsqueeze(0).broadcast_to([8, 4, T // 4])
-            nc.sync.dma_start(x_bytes[32 * q : 32 * q + 32, :].bitcast(I32), rows)
+        for q in range(P // QUADRANT):
+            rows = x_scales[0].bitcast(I32)[4 * q : 4 * q + 4, :].unsqueeze(0).broadcast_to([QUADRANT // 4, 4, T // 4])
+            nc.sync.dma_start(x_bytes[QUADRANT * q : QUADRANT * (q + 1), :].bitcast(I32), rows)
         x_tab = load_words("x_tab", x_words, T)
         d_tab = load_words("d_tab", d_words, G)
-        load_list("k2", k2)
-        load_list("two", two)
-        load_list("n1", n1)
-        load_list("n2", n2)
-        load_list("n3", n3)
-        load_list("n4", n4)
-        load_list("n5", n5)
-        load_list("n6", n6)
+        for name, src in (("k2", k2), ("two", two), ("n1", n1), ("n2", n2), ("n3", n3), ("n4", n4), ("n5", n5), ("n6", n6)):
+            load_list(name, src)
 
-        def coded_product(side, code_list, token_list, offsets, queue):
-            d_b = picked.tile([P, H], U8, name="d_b" + side, align_bytes=64, offset=offsets[0])
-            x_b = picked.tile([P, S], U8, name="x_b" + side, align_bytes=64, offset=offsets[1])
-            x_w = picked.tile([P, S], U32, name="x_w" + side, align_bytes=64, offset=offsets[2])
-            d_w = picked.tile([P, H], U32, name="d_w" + side, align_bytes=64, offset=offsets[3])
-            planes = work.tile([P, H], U8, name="planes" + side, align_bytes=64)
+        def entries(name, first, count):
+            return lists[name][:, first // GROUP : (first + count) // GROUP]
+
+        def coded_product(side, code_list, token_list, place, queue):
+            d_b = picked.tile([P, H], U8, name="d_b" + side, align_bytes=64, offset=place["d_b"])
+            x_b = picked.tile([P, S], U8, name="x_b" + side, align_bytes=64, offset=place["x_b"])
+            x_w = picked.tile([P, S], U32, name="x_w" + side, align_bytes=64, offset=place["x_w"])
+            d_w = [
+                picked.tile([P, H // 2], U32, name="d_w%s%d" % (side, u), align_bytes=64, offset=place["d_w"][u])
+                for u in range(2)
+            ]
+            d_scale = work.tile([P, H], U8, name="planes" + side, align_bytes=64)
             dealt = work.tile([P, H], U32, name="dealt" + side, align_bytes=64)
+
             nc.vector.tensor_copy(d_b[:], d_bytes[:].indirect(lists[code_list][:]))
             nc.vector.tensor_copy(
-                planes[:].bitcast(I32).rearrange("p (t b q) -> p t b q", t=PACK, q=2),
-                d_b[:].bitcast(I32).rearrange("p (b t q) -> p t b q", t=PACK, q=2),
+                d_scale[:].bitcast(I32).rearrange("p (t b q) -> p t b q", t=TILES, q=RUN // 4),
+                d_b[:].bitcast(I32).rearrange("p (b t q) -> p t b q", t=TILES, q=RUN // 4),
             )
-            for c in range(1, 4):
-                queue.dma_start(planes[c:P:32, :].bitcast(I32), planes[8 * c : P : 32, :].bitcast(I32))
+            for i in range(1, 4):
+                queue.dma_start(d_scale[i:P:QUADRANT, :].bitcast(I32), d_scale[RUN * i : P : QUADRANT, :].bitcast(I32))
             nc.vector.tensor_copy(x_b[:], x_bytes[:].indirect(lists[token_list][:]))
             nc.vector.tensor_copy(x_w[:], x_tab[:].bitcast(U32).indirect(lists[token_list][:]))
-            nc.vector.tensor_copy(d_w[:], d_tab[:].bitcast(U32).indirect(lists[code_list][:]))
-            nc.vector.tensor_copy(
-                dealt[:].rearrange("p (t b q) -> p t b q", t=PACK, q=8),
-                d_w[:].rearrange("p (b t q) -> p t b q", t=PACK, q=8),
-            )
+            for u in range(2):
+                nc.vector.tensor_copy(d_w[u][:], d_tab[:].bitcast(U32).indirect(entries(code_list, u * H // 2, H // 2)))
+            for u in range(2):
+                blocks = slice(u * BLOCKS // 2, (u + 1) * BLOCKS // 2)
+                nc.vector.tensor_copy(
+                    dealt[:].rearrange("p (t b q) -> p t b q", t=TILES, q=RUN)[:, :, blocks, :],
+                    d_w[u][:].rearrange("p (b t q) -> p t b q", t=TILES, q=RUN),
+                )
             banks = []
-            for t in range(PACK):
+            for t in range(TILES):
                 bank = psum.tile([P, S], F32, name="bank", tag="bank")
                 cols = slice(t * P, (t + 1) * P)
                 nc.tensor.matmul_mx(
                     out=bank[:],
                     lhsT=dealt[:, cols].bitcast(FP8X4),
-                    lhsT_scale=planes[:, cols],
+                    lhsT_scale=d_scale[:, cols],
                     rhs=x_w[:].bitcast(FP8X4),
                     rhs_scale=x_b[:],
                     start=True,
@@ -107,69 +117,62 @@ def tile_picked_twpqpathbhaar_none_p_kernel(
             return banks
 
         def leave_psum(side, banks, t):
-            tile = work.tile([P, S], F32, name="rows_%s%d" % (side, t), tag="rows_%s%d" % (side, t), align_bytes=64)
+            name = "rows_%s%d" % (side, t)
+            tile = work.tile([P, S], F32, name=name, tag=name, align_bytes=64)
             nc.scalar.activation(tile[:], banks[t][:], COPY, scale=0.0625)
             return tile
 
-        a_banks = coded_product("a", "k1", "offs", (0, 512, 8192, 4608), nc.scalar)
-        b_banks = coded_product("b", "k2", "two", (5120, 5632, 6144, 3072), nc.sync)
+        a_banks = coded_product("a", "k1", "offs", PLACE_A, nc.scalar)
+        b_banks = coded_product("b", "k2", "two", PLACE_B, nc.sync)
 
-        w_raw = picked.tile([P, PACK, N], F32, align_bytes=64, offset=8192)
-        for j in range(PACK):
-            nc.sync.dma_start(w_raw[:, j, :], w1.rearrange("(b t q) n -> t b q n", t=PACK, q=8)[j])
-        gain = picked.tile([P, PACK, 8], F32, align_bytes=64, offset=512)
-        for t in range(PACK):
+        w_raw = picked.tile([P, TILES, N], F32, align_bytes=64, offset=PLACE_A["x_w"])
+        for t in range(TILES):
+            nc.sync.dma_start(w_raw[:, t, :], w1.rearrange("(b t q) n -> t b q n", t=TILES, q=RUN)[t])
+        gain = picked.tile([P, TILES, 8], F32, align_bytes=64, offset=PLACE_A["x_b"])
+        for t in range(TILES):
             with nc.allow_non_contiguous_dma(reason="one gain a partition"):
-                nc.sync.dma_start(gain[:, t, 0:1], gn.rearrange("(b t q) o -> t b q o", t=PACK, q=8)[t])
+                nc.sync.dma_start(gain[:, t, 0:1], gn.rearrange("(b t q) o -> t b q o", t=TILES, q=RUN)[t])
 
-        a_rows = [leave_psum("a", a_banks, t) for t in range(PACK)]
-
-
-        pairs = (("n1", "n3"), ("n2", "n4"))
-
-        def entries(name, c0, cw):
-            return lists[name][:, c0 // 16 : (c0 + cw) // 16]
+        a_rows = [leave_psum("a", a_banks, t) for t in range(TILES)]
 
         a_picked = {}
 
         def pick_a(c, t, e):
-            c0, cw = CHUNKS[c]
-            window = a_rows[t][:].indirect(entries(pairs[e][0], c0, cw))
-            if t == PACK - 1:
-                tile = picked.tile([P, cw], F32, name="a_pick%d%d" % (t, e), offset=3072 + 1024 * e)
+            window = a_rows[t][:].indirect(entries(SUM_LISTS[e][0], c * CHUNK, CHUNK))
+            if t == LAST_TILE:
+                tile = picked.tile([P, CHUNK], F32, name="a_pick%d%d" % (t, e), offset=PLACE_B["d_w"][e])
             else:
-                tile = work.tile([P, cw], F32, name="a_pick%d%d" % (t, e))
-            if c == 0 and t == PACK - 1:
+                tile = work.tile([P, CHUNK], F32, name="a_pick%d%d" % (t, e))
+            if c == 0 and t == LAST_TILE:
                 nc.vector.tensor_copy(tile[:], window)
             else:
                 nc.scalar.activation(tile[:], window, COPY)
             a_picked[c, t, e] = tile
 
-        for t in (3, 0, 1):
+        for t in (LAST_TILE, 0, 1):
             for e in range(2):
                 pick_a(0, t, e)
         b_rows = [leave_psum("b", b_banks, t) for t in range(2)]
         for e in range(2):
             pick_a(0, 2, e)
-        b_rows.extend(leave_psum("b", b_banks, t) for t in range(2, PACK))
+        b_rows.extend(leave_psum("b", b_banks, t) for t in range(2, TILES))
 
-        w_by_tile = w_raw[:].rearrange("p j (b t q) -> p t b q j", t=PACK, q=8)
-        w_grouped = picked.tile([P, PACK * P], BF16, align_bytes=64, offset=6144)
-        nc.scalar.copy(w_grouped[:].rearrange("p (b q j) -> p b q j", q=8, j=PACK), w_by_tile[:, 0])
+        w_by_tile = w_raw[:].rearrange("p j (b t q) -> p t b q j", t=TILES, q=RUN)
+        w_grouped = picked.tile([P, TILES * P], BF16, align_bytes=64, offset=PLACE_B["x_w"])
+        nc.scalar.copy(w_grouped[:].rearrange("p (b q j) -> p b q j", q=RUN, j=TILES), w_by_tile[:, 0])
         w_codes = {0: work.tile([P, P], U32, name="w_codes0", align_bytes=64)}
-        w_scales = work.tile([P, P], U8, align_bytes=64)
-        w_planes = {0: w_scales}
+        w_scales = {0: work.tile([P, P], U8, name="w_scales", align_bytes=64)}
 
         z_codes = work.tile([P, S], U32, align_bytes=64)
         z_scales = work.tile([P, S], U8, align_bytes=64)
-        h_rows = [work.tile([P, S], F32, name="h_rows%d" % t) for t in range(PACK)]
+        h_rows = [work.tile([P, S], F32, name="h_rows%d" % t) for t in range(TILES)]
 
         def dense(t, cols):
             bank = psum.tile([P, cols.stop - cols.start], F32, name="bank", tag="bank")
             nc.tensor.matmul_mx(
                 out=bank[:],
                 lhsT=w_codes[t][:, 0:P].bitcast(FP8X4),
-                lhsT_scale=w_planes[t][:, 0:P],
+                lhsT_scale=w_scales[t][:, 0:P],
                 rhs=z_codes[:, cols].bitcast(FP8X4),
                 rhs_scale=z_scales[:, cols],
                 start=True,
@@ -177,69 +180,88 @@ def tile_picked_twpqpathbhaar_none_p_kernel(
             )
             return bank
 
-        first_banks = []
-        for c, (c0, cw) in enumerate(CHUNKS):
-            last = c == len(CHUNKS) - 1
-            halves = [slice(0, cw // 2), slice(cw // 2, cw)]
-            sums = work.tile([P, 2, PACK, cw], F32, name="sums%d" % c)
-            larger = work.tile([P, PACK, cw], F32, name="larger%d" % c)
-            for t in range(PACK):
-                for e in range(2):
-                    if c > 0:
-                        pick_a(c, t, e)
-                    window = b_rows[t][:].indirect(entries(pairs[e][1], c0, cw))
-                    if last and 2 * t + e >= 2 * PACK - BOTH_ON_SCALAR:
-                        b_pick = work.tile([P, cw], F32, name="b_pick%d%d" % (t, e))
-                        nc.scalar.activation(b_pick[:], window, COPY)
-                        for part in halves if (t, e) == (PACK - 1, 1) else [slice(0, cw)]:
-                            nc.vector.tensor_tensor(sums[:, e, t, part], b_pick[:, part], a_picked[c, t, e][:, part], ADD)
-                    else:
-                        nc.vector.tensor_tensor(sums[:, e, t, :], window, a_picked[c, t, e][:], ADD)
-                if last and t == PACK - 2:
-                    nc.vector.tensor_tensor(larger[:, 0 : t + 1, :], sums[:, 0, 0 : t + 1, :], sums[:, 1, 0 : t + 1, :], MAX)
-            first = PACK - 1 if last else 0
-            for part in halves:
-                nc.vector.tensor_tensor(larger[:, first:, part], sums[:, 0, first:, part], sums[:, 1, first:, part], MAX)
-            z_grouped = work.tile([P, cw, PACK], BF16, name="z_grouped%d" % c, tag="z_grouped%d" % c, align_bytes=64)
-            for part in halves:
+        def b_window(c, t, e):
+            return b_rows[t][:].indirect(entries(SUM_LISTS[e][1], c * CHUNK, CHUNK))
+
+        def columns(c, part):
+            return slice(c * CHUNK + part.start, c * CHUNK + part.stop)
+
+        def larger_of(larger, sums, tiles, part):
+            nc.vector.tensor_tensor(larger[:, tiles, part], sums[:, 0, tiles, part], sums[:, 1, tiles, part], MAX)
+
+        def times_gain(c, larger):
+            name = "z_grouped%d" % c
+            z_grouped = work.tile([P, CHUNK, TILES], BF16, name=name, tag=name, align_bytes=64)
+            for part in HALVES:
                 nc.vector.tensor_tensor(
                     z_grouped[:, part, :].rearrange("p (c i) t -> p c t i", i=4),
                     larger[:, :, part].rearrange("p t (c i) -> p c t i", i=4),
-                    gain[:, :, 0:1].unsqueeze(1).broadcast_to([P, cw // 8, PACK, 4]),
+                    gain[:, :, 0:1].unsqueeze(1).broadcast_to([P, CHUNK // 2 // 4, TILES, 4]),
                     MULT,
                 )
-            if c == 0:
-                nc.vector.quantize_mx(w_codes[0][:].bitcast(FP8X4), w_scales[:, 0:P], w_grouped[:])
-            for part in halves:
-                cols = slice(c0 + part.start, c0 + part.stop)
+            return z_grouped
+
+        def quantise_z(c, z_grouped):
+            for part in HALVES:
+                cols = columns(c, part)
                 nc.vector.quantize_mx(
                     z_codes[:, cols].bitcast(FP8X4), z_scales[:, cols], z_grouped[:, part, :].rearrange("p c t -> p (c t)")
                 )
-            for part in halves if last else [slice(0, cw)]:
-                cols = slice(c0 + part.start, c0 + part.stop)
-                first_banks.append((cols, dense(0, cols)))
-            if not last:
-                nc.scalar.copy(h_rows[0][:, cols], first_banks.pop()[1][:])
-        w_rest_grouped = work.tile([P, PACK * (N - P)], BF16, tag="rows_b3", align_bytes=64)
+
+        whole = slice(0, CHUNK)
+
+        sums = work.tile([P, 2, TILES, CHUNK], F32, name="sums0")
+        larger = work.tile([P, TILES, CHUNK], F32, name="larger0")
+        for t in range(TILES):
+            for e in range(2):
+                nc.vector.tensor_tensor(sums[:, e, t, :], b_window(0, t, e), a_picked[0, t, e][:], ADD)
+        for part in HALVES:
+            larger_of(larger, sums, slice(0, TILES), part)
+        z_grouped = times_gain(0, larger)
+        nc.vector.quantize_mx(w_codes[0][:].bitcast(FP8X4), w_scales[0][:, 0:P], w_grouped[:])
+        quantise_z(0, z_grouped)
+        nc.scalar.copy(h_rows[0][:, columns(0, whole)], dense(0, columns(0, whole))[:])
+
+        sums = work.tile([P, 2, TILES, CHUNK], F32, name="sums1")
+        larger = work.tile([P, TILES, CHUNK], F32, name="larger1")
+        for t in range(TILES):
+            for e in range(2):
+                pick_a(1, t, e)
+                if t < FUSED_TILES:
+                    nc.vector.tensor_tensor(sums[:, e, t, :], b_window(1, t, e), a_picked[1, t, e][:], ADD)
+                else:
+                    b_pick = work.tile([P, CHUNK], F32, name="b_pick%d%d" % (t, e))
+                    nc.scalar.activation(b_pick[:], b_window(1, t, e), COPY)
+                    for part in HALVES if (t, e) == (LAST_TILE, 1) else [whole]:
+                        nc.vector.tensor_tensor(sums[:, e, t, part], b_pick[:, part], a_picked[1, t, e][:, part], ADD)
+            if t == LAST_TILE - 1:
+                larger_of(larger, sums, slice(0, LAST_TILE), whole)
+        for part in HALVES:
+            larger_of(larger, sums, slice(LAST_TILE, TILES), part)
+        z_grouped = times_gain(1, larger)
+        quantise_z(1, z_grouped)
+        first_banks = [dense(0, columns(1, part)) for part in HALVES]
+
+        w_rest_grouped = work.tile([P, TILES * (N - P)], BF16, tag="rows_b%d" % LAST_TILE, align_bytes=64)
         nc.scalar.copy(
-            w_rest_grouped[:].rearrange("p (t b q j) -> p t b q j", t=PACK - 1, q=8, j=PACK), w_by_tile[:, 1:PACK]
+            w_rest_grouped[:].rearrange("p (t b q j) -> p t b q j", t=TILES - 1, q=RUN, j=TILES), w_by_tile[:, 1:TILES]
         )
-        for cols, bank in first_banks:
-            nc.scalar.copy(h_rows[0][:, cols], bank[:])
-        w_rest = work.tile([P, N - P], U32, tag="z_grouped%d" % (len(CHUNKS) - 1), align_bytes=64)
+        for part, bank in zip(HALVES, first_banks):
+            nc.scalar.copy(h_rows[0][:, columns(1, part)], bank[:])
+        w_rest = work.tile([P, N - P], U32, tag="z_grouped1", align_bytes=64)
         w_rest_scales = work.tile([P, N - P], U8, align_bytes=64)
         nc.vector.quantize_mx(w_rest[:].bitcast(FP8X4), w_rest_scales[:], w_rest_grouped[:])
-        for t in range(1, PACK):
+        for t in range(1, TILES):
             w_codes[t] = w_rest[:, (t - 1) * P : t * P]
-            w_planes[t] = w_rest_scales[:, (t - 1) * P : t * P]
-        last_banks = {t: dense(t, slice(0, S)) for t in range(1, PACK)}
+            w_scales[t] = w_rest_scales[:, (t - 1) * P : t * P]
+        h_banks = {t: dense(t, slice(0, S)) for t in range(1, TILES)}
 
-        out_rows = out.rearrange("(b t q) n -> t b q n", t=PACK, q=8)
+        out_rows = out.rearrange("(b t q) n -> t b q n", t=TILES, q=RUN)
         pa, pb_neg, placed = {}, {}, {}
 
-        def differences(t):
+        def place_rb(t):
             if t > 0:
-                nc.scalar.copy(h_rows[t][:], last_banks[t][:])
+                nc.scalar.copy(h_rows[t][:], h_banks[t][:])
             pa[t] = work.tile([P, W], F32, name="pa%d" % t)
             pb_neg[t] = work.tile([P, W], F32, name="pb_neg%d" % t)
             nc.scalar.activation(pa[t][:], h_rows[t][:].indirect(lists["n5"][:]), COPY)
@@ -250,22 +272,20 @@ def tile_picked_twpqpathbhaar_none_p_kernel(
             placed[t] = work.tile([P, S], F32, name="placed%d" % t)
             nc.vector.tensor_tensor(placed[t][:].indirect(lists["n6"][:]), pa[t][:], pb_neg[t][:], ADD)
 
-        def sums_out(t):
+        def place_ra(t):
             qa = work.tile([P, W], F32, name="qa%d" % t)
             qb = work.tile([P, W], F32, name="qb%d" % t)
             nc.scalar.activation(qa[:], pa[t][:], COPY, scale=0.75)
             nc.scalar.activation(qb[:], pb_neg[t][:], COPY, scale=-0.75)
             nc.vector.tensor_tensor(placed[t][:].indirect(lists["n5"][:]), qa[:], qb[:], ADD)
-            if t < PACK - 1:
+            if t < LAST_TILE:
                 nc.sync.dma_start(out_rows[t], placed[t][:])
             else:
                 nc.sync.dma_start(out_rows[t][:, :, 0:W], placed[t][:, 0:W])
                 nc.scalar.dma_start(out_rows[t][:, :, W:S], placed[t][:, W:S])
 
-        differences(0)
-        sums_out(0)
-        differences(1)
-        for t in range(1, PACK):
-            if t + 1 < PACK:
-                differences(t + 1)
-            sums_out(t)
+        place_rb(0)
+        for t in range(TILES):
+            if t < LAST_TILE:
+                place_rb(t + 1)
+            place_ra(t)

from contextlib import ExitStack

import concourse.mybir as mybir

K, T, S, N, G, H, W = 512, 1024, 512, 512, 2048, 512, 256
FLOPS = 2 * (K * H * S + K * H * S + H * N * S)

F32 = mybir.dt.float32
BF16 = mybir.dt.bfloat16
I32 = mybir.dt.int32
U32 = mybir.dt.uint32
U16 = mybir.dt.uint16
U8 = mybir.dt.uint8
FP8X4 = mybir.dt.float8_e4m3fn_x4
COPY = mybir.ActivationFunctionType.Copy
ADD = mybir.AluOpType.add
MULT = mybir.AluOpType.mult
MAX = mybir.AluOpType.max

P = 128
TILES = 4
LAST_TILE = TILES - 1
BLOCKS = 16
RUN = 8
QUADRANT = 32
GROUP = 16
CHUNK = 256
HALVES = (slice(0, CHUNK // 2), slice(CHUNK // 2, CHUNK))
SUM_LISTS = (("n1", "n3"), ("n2", "n4"))
FUSED_TILES = 1

PLACE_A = {"d_b": 0, "x_b": 512, "x_w": 8320, "d_w": (4096, 6144)}
PLACE_B = {"d_b": 4160, "x_b": 5696, "x_w": 6208, "d_w": (3136, 4672)}


def tile_picked_twpqpathbhaar_none_p_kernel(
    tc, x_words, x_scales, d_words, d_scales, gn, w1, offs, k1, two, k2, n1, n2, n3, n4, n5, n6, out
):
    nc = tc.nc
    with ExitStack() as ctx:
        held = ctx.enter_context(tc.tile_pool(name="held", bufs=1))
        picked = ctx.enter_context(tc.tile_pool(name="picked", bufs=1))
        work = ctx.enter_context(tc.tile_pool(name="work", bufs=1))
        psum = ctx.enter_context(tc.psum_pool(name="psum", bufs=8))

        lists = {}

        def load_list(name, src):
            lists[name] = held.tile(list(src.shape), U16, name="list_" + name)
            nc.sync.dma_start(lists[name][:], src)

        def load_words(name, src, cols):
            tile = held.tile([P, cols], I32, name=name, align_bytes=64)
            nc.sync.dma_start(tile[:], src[0].rearrange("p c r -> p (c r)").bitcast(I32))
            return tile

        load_list("k1", k1)
        d_bytes = held.tile([P, G], U8, align_bytes=64)
        nc.sync.dma_start(
            d_bytes[:].bitcast(I32), d_scales[0].bitcast(I32).unsqueeze(1).broadcast_to([BLOCKS, RUN, G // 4])
        )
        load_list("offs", offs)
        x_bytes = held.tile([P, T], U8, align_bytes=64)
        for q in range(P // QUADRANT):
            rows = x_scales[0].bitcast(I32)[4 * q : 4 * q + 4, :].unsqueeze(0).broadcast_to([QUADRANT // 4, 4, T // 4])
            nc.sync.dma_start(x_bytes[QUADRANT * q : QUADRANT * (q + 1), :].bitcast(I32), rows)
        x_tab = load_words("x_tab", x_words, T)
        d_tab = load_words("d_tab", d_words, G)
        for name, src in (("k2", k2), ("two", two), ("n1", n1), ("n2", n2), ("n3", n3), ("n4", n4), ("n5", n5), ("n6", n6)):
            load_list(name, src)

        def entries(name, first, count):
            return lists[name][:, first // GROUP : (first + count) // GROUP]

        def coded_product(side, code_list, token_list, place, queue):
            d_b = picked.tile([P, H], U8, name="d_b" + side, align_bytes=64, offset=place["d_b"])
            x_b = picked.tile([P, S], U8, name="x_b" + side, align_bytes=64, offset=place["x_b"])
            x_w = picked.tile([P, S], U32, name="x_w" + side, align_bytes=64, offset=place["x_w"])
            d_w = [
                picked.tile([P, H // 2], U32, name="d_w%s%d" % (side, u), align_bytes=64, offset=place["d_w"][u])
                for u in range(2)
            ]
            d_scale = work.tile([P, H], U8, name="planes" + side, align_bytes=64)
            dealt = work.tile([P, H], U32, name="dealt" + side, align_bytes=64)

            nc.vector.tensor_copy(d_b[:], d_bytes[:].indirect(lists[code_list][:]))
            nc.vector.tensor_copy(
                d_scale[:].bitcast(I32).rearrange("p (t b q) -> p t b q", t=TILES, q=RUN // 4),
                d_b[:].bitcast(I32).rearrange("p (b t q) -> p t b q", t=TILES, q=RUN // 4),
            )
            for i in range(1, 4):
                queue.dma_start(d_scale[i:P:QUADRANT, :].bitcast(I32), d_scale[RUN * i : P : QUADRANT, :].bitcast(I32))
            nc.vector.tensor_copy(x_b[:], x_bytes[:].indirect(lists[token_list][:]))
            nc.vector.tensor_copy(x_w[:], x_tab[:].bitcast(U32).indirect(lists[token_list][:]))
            for u in range(2):
                nc.vector.tensor_copy(d_w[u][:], d_tab[:].bitcast(U32).indirect(entries(code_list, u * H // 2, H // 2)))
            for u in range(2):
                blocks = slice(u * BLOCKS // 2, (u + 1) * BLOCKS // 2)
                nc.vector.tensor_copy(
                    dealt[:].rearrange("p (t b q) -> p t b q", t=TILES, q=RUN)[:, :, blocks, :],
                    d_w[u][:].rearrange("p (b t q) -> p t b q", t=TILES, q=RUN),
                )
            banks = []
            for t in range(TILES):
                bank = psum.tile([P, S], F32, name="bank", tag="bank")
                cols = slice(t * P, (t + 1) * P)
                nc.tensor.matmul_mx(
                    out=bank[:],
                    lhsT=dealt[:, cols].bitcast(FP8X4),
                    lhsT_scale=d_scale[:, cols],
                    rhs=x_w[:].bitcast(FP8X4),
                    rhs_scale=x_b[:],
                    start=True,
                    stop=True,
                )
                banks.append(bank)
            return banks

        def leave_psum(side, banks, t):
            name = "rows_%s%d" % (side, t)
            tile = work.tile([P, S], F32, name=name, tag=name, align_bytes=64)
            nc.scalar.activation(tile[:], banks[t][:], COPY, scale=0.0625)
            return tile

        a_banks = coded_product("a", "k1", "offs", PLACE_A, nc.scalar)
        b_banks = coded_product("b", "k2", "two", PLACE_B, nc.sync)

        w_raw = picked.tile([P, TILES, N], F32, align_bytes=64, offset=PLACE_A["x_w"])
        for t in range(TILES):
            nc.sync.dma_start(w_raw[:, t, :], w1.rearrange("(b t q) n -> t b q n", t=TILES, q=RUN)[t])
        gain = picked.tile([P, TILES, 8], F32, align_bytes=64, offset=PLACE_A["x_b"])
        for t in range(TILES):
            with nc.allow_non_contiguous_dma(reason="one gain a partition"):
                nc.sync.dma_start(gain[:, t, 0:1], gn.rearrange("(b t q) o -> t b q o", t=TILES, q=RUN)[t])

        a_rows = [leave_psum("a", a_banks, t) for t in range(TILES)]

        a_picked = {}

        def pick_a(c, t, e):
            window = a_rows[t][:].indirect(entries(SUM_LISTS[e][0], c * CHUNK, CHUNK))
            if t == LAST_TILE:
                tile = picked.tile([P, CHUNK], F32, name="a_pick%d%d" % (t, e), offset=PLACE_B["d_w"][e])
            else:
                tile = work.tile([P, CHUNK], F32, name="a_pick%d%d" % (t, e))
            if c == 0 and t == LAST_TILE:
                nc.vector.tensor_copy(tile[:], window)
            else:
                nc.scalar.activation(tile[:], window, COPY)
            a_picked[c, t, e] = tile

        for t in (LAST_TILE, 0, 1):
            for e in range(2):
                pick_a(0, t, e)
        b_rows = [leave_psum("b", b_banks, t) for t in range(2)]
        for e in range(2):
            pick_a(0, 2, e)
        b_rows.extend(leave_psum("b", b_banks, t) for t in range(2, TILES))

        w_by_tile = w_raw[:].rearrange("p j (b t q) -> p t b q j", t=TILES, q=RUN)
        w_grouped = picked.tile([P, TILES * P], BF16, align_bytes=64, offset=PLACE_B["x_w"])
        nc.scalar.copy(w_grouped[:].rearrange("p (b q j) -> p b q j", q=RUN, j=TILES), w_by_tile[:, 0])
        w_codes = {0: work.tile([P, P], U32, name="w_codes0", align_bytes=64)}
        w_scales = {0: work.tile([P, P], U8, name="w_scales", align_bytes=64)}

        z_codes = work.tile([P, S], U32, align_bytes=64)
        z_scales = work.tile([P, S], U8, align_bytes=64)
        h_rows = [work.tile([P, S], F32, name="h_rows%d" % t) for t in range(TILES)]

        def dense(t, cols):
            bank = psum.tile([P, cols.stop - cols.start], F32, name="bank", tag="bank")
            nc.tensor.matmul_mx(
                out=bank[:],
                lhsT=w_codes[t][:, 0:P].bitcast(FP8X4),
                lhsT_scale=w_scales[t][:, 0:P],
                rhs=z_codes[:, cols].bitcast(FP8X4),
                rhs_scale=z_scales[:, cols],
                start=True,
                stop=True,
            )
            return bank

        def b_window(c, t, e):
            return b_rows[t][:].indirect(entries(SUM_LISTS[e][1], c * CHUNK, CHUNK))

        def columns(c, part):
            return slice(c * CHUNK + part.start, c * CHUNK + part.stop)

        def larger_of(larger, sums, tiles, part):
            nc.vector.tensor_tensor(larger[:, tiles, part], sums[:, 0, tiles, part], sums[:, 1, tiles, part], MAX)

        def times_gain(c, larger):
            name = "z_grouped%d" % c
            z_grouped = work.tile([P, CHUNK, TILES], BF16, name=name, tag=name, align_bytes=64)
            for part in HALVES:
                nc.vector.tensor_tensor(
                    z_grouped[:, part, :].rearrange("p (c i) t -> p c t i", i=4),
                    larger[:, :, part].rearrange("p t (c i) -> p c t i", i=4),
                    gain[:, :, 0:1].unsqueeze(1).broadcast_to([P, CHUNK // 2 // 4, TILES, 4]),
                    MULT,
                )
            return z_grouped

        def quantise_z(c, z_grouped):
            for part in HALVES:
                cols = columns(c, part)
                nc.vector.quantize_mx(
                    z_codes[:, cols].bitcast(FP8X4), z_scales[:, cols], z_grouped[:, part, :].rearrange("p c t -> p (c t)")
                )

        whole = slice(0, CHUNK)

        sums = work.tile([P, 2, TILES, CHUNK], F32, name="sums0")
        larger = work.tile([P, TILES, CHUNK], F32, name="larger0")
        for t in range(TILES):
            for e in range(2):
                nc.vector.tensor_tensor(sums[:, e, t, :], b_window(0, t, e), a_picked[0, t, e][:], ADD)
        for part in HALVES:
            larger_of(larger, sums, slice(0, TILES), part)
        z_grouped = times_gain(0, larger)
        nc.vector.quantize_mx(w_codes[0][:].bitcast(FP8X4), w_scales[0][:, 0:P], w_grouped[:])
        quantise_z(0, z_grouped)
        nc.scalar.copy(h_rows[0][:, columns(0, whole)], dense(0, columns(0, whole))[:])

        sums = work.tile([P, 2, TILES, CHUNK], F32, name="sums1")
        larger = work.tile([P, TILES, CHUNK], F32, name="larger1")
        for t in range(TILES):
            for e in range(2):
                pick_a(1, t, e)
                if t < FUSED_TILES:
                    nc.vector.tensor_tensor(sums[:, e, t, :], b_window(1, t, e), a_picked[1, t, e][:], ADD)
                else:
                    b_pick = work.tile([P, CHUNK], F32, name="b_pick%d%d" % (t, e))
                    nc.scalar.activation(b_pick[:], b_window(1, t, e), COPY)
                    for part in HALVES if (t, e) == (LAST_TILE, 1) else [whole]:
                        nc.vector.tensor_tensor(sums[:, e, t, part], b_pick[:, part], a_picked[1, t, e][:, part], ADD)
            if t == LAST_TILE - 1:
                larger_of(larger, sums, slice(0, LAST_TILE), whole)
        for part in HALVES:
            larger_of(larger, sums, slice(LAST_TILE, TILES), part)
        z_grouped = times_gain(1, larger)
        quantise_z(1, z_grouped)
        first_banks = [dense(0, columns(1, part)) for part in HALVES]

        w_rest_grouped = work.tile([P, TILES * (N - P)], BF16, tag="rows_b%d" % LAST_TILE, align_bytes=64)
        nc.scalar.copy(
            w_rest_grouped[:].rearrange("p (t b q j) -> p t b q j", t=TILES - 1, q=RUN, j=TILES), w_by_tile[:, 1:TILES]
        )
        for part, bank in zip(HALVES, first_banks):
            nc.scalar.copy(h_rows[0][:, columns(1, part)], bank[:])
        w_rest = work.tile([P, N - P], U32, tag="z_grouped1", align_bytes=64)
        w_rest_scales = work.tile([P, N - P], U8, align_bytes=64)
        nc.vector.quantize_mx(w_rest[:].bitcast(FP8X4), w_rest_scales[:], w_rest_grouped[:])
        for t in range(1, TILES):
            w_codes[t] = w_rest[:, (t - 1) * P : t * P]
            w_scales[t] = w_rest_scales[:, (t - 1) * P : t * P]
        h_banks = {t: dense(t, slice(0, S)) for t in range(1, TILES)}

        out_rows = out.rearrange("(b t q) n -> t b q n", t=TILES, q=RUN)
        pa, pb_neg, placed = {}, {}, {}

        def place_rb(t):
            if t > 0:
                nc.scalar.copy(h_rows[t][:], h_banks[t][:])
            pa[t] = work.tile([P, W], F32, name="pa%d" % t)
            pb_neg[t] = work.tile([P, W], F32, name="pb_neg%d" % t)
            nc.scalar.activation(pa[t][:], h_rows[t][:].indirect(lists["n5"][:]), COPY)
            if t == 0:
                nc.vector.tensor_scalar(pb_neg[t][:], h_rows[t][:].indirect(lists["n6"][:]), -1.0, 0.0, MULT, ADD)
            else:
                nc.scalar.activation(pb_neg[t][:], h_rows[t][:].indirect(lists["n6"][:]), COPY, scale=-1.0)
            placed[t] = work.tile([P, S], F32, name="placed%d" % t)
            nc.vector.tensor_tensor(placed[t][:].indirect(lists["n6"][:]), pa[t][:], pb_neg[t][:], ADD)

        def place_ra(t):
            qa = work.tile([P, W], F32, name="qa%d" % t)
            qb = work.tile([P, W], F32, name="qb%d" % t)
            nc.scalar.activation(qa[:], pa[t][:], COPY, scale=0.75)
            nc.scalar.activation(qb[:], pb_neg[t][:], COPY, scale=-0.75)
            nc.vector.tensor_tensor(placed[t][:].indirect(lists["n5"][:]), qa[:], qb[:], ADD)
            if t < LAST_TILE:
                nc.sync.dma_start(out_rows[t], placed[t][:])
            else:
                nc.sync.dma_start(out_rows[t][:, :, 0:W], placed[t][:, 0:W])
                nc.scalar.dma_start(out_rows[t][:, :, W:S], placed[t][:, W:S])

        place_rb(0)
        for t in range(TILES):
            if t < LAST_TILE:
                place_rb(t + 1)
            place_ra(t)
